import numpy as np
import ml_dtypes


def mxq(x, axis, fmt="e4m3"):
    dtype, down = {"e4m3": (ml_dtypes.float8_e4m3fn, 7), "e5m2": (ml_dtypes.float8_e5m2, 14)}[fmt]
    v = np.moveaxis(np.asarray(x, np.float32).astype(ml_dtypes.bfloat16).astype(np.float64), axis, -1)
    blocks = v.reshape(v.shape[:-1] + (-1, 32))
    amax = np.abs(blocks).max(-1, keepdims=True)
    byte = np.maximum(np.where(amax > 0, np.frexp(amax)[1] - 1 + 127, 0) - down, 1)
    scale = np.exp2(byte - 127.0)
    codes = (blocks / scale).astype(np.float32).astype(dtype).astype(np.float64)
    return np.moveaxis((codes * scale).reshape(v.shape), -1, axis)


WIDE = False


def mx_kscale(k):
    if not WIDE:
        return np.ones(k)
    levels = np.array([10, -10, 5, -5, 0])
    if k % 512:
        return np.exp2(np.random.permutation(np.resize(levels, k // 32))).repeat(32)
    a = np.empty((k // 512, 16))
    for p in range(k // 512):
        a[p, :8] = np.random.permutation(np.resize(levels, 8))
        for g in range(8):
            far = levels[np.abs(levels - a[p, g]) >= 10]
            a[p, g + 8] = far[np.random.randint(len(far))]
    return np.exp2(a.ravel()).repeat(32)


def f64(x):
    return np.asarray(x).astype(np.float64)


def striped(idx):
    return np.tile(idx.reshape(-1, 16).T, (8, 1)).astype(np.uint16)


def unstriped(offs):
    return offs[:16].T.reshape(-1).astype(np.int64)


def sigmoid(v):
    return 1.0 / (1.0 + np.exp(-np.maximum(v, -700.0)))


K, T, E, C, H, N = 512, 1024, 8, 128, 512, 256
TOP = 4
PAD = 64


def by_expert(wq, xq):
    return np.concatenate([wq[e].T @ xq[:, e * C:(e + 1) * C] for e in range(E)], axis=1)


def setup_inputs():
    n = np.random.standard_normal
    s = mx_kscale(K)[:, None]
    u = mx_kscale(H)
    slot_token = np.empty(E * C, np.int64); pos = np.tile(E * C + np.arange(T) % PAD, (TOP, 1)); taken = np.zeros(T, np.int64)
    liked = np.random.randn(T)
    for e in np.random.permutation(E):
        free = np.flatnonzero(taken < TOP); pick = np.random.permutation(free[np.argsort(-(liked[free] + np.random.gumbel(size=free.size)))[:C]]); slot_token[e * C:(e + 1) * C] = pick
        pos[taken[pick], pick] = e * C + np.arange(C); taken[pick] += 1
    g = np.random.uniform(0.2, 0.8, (TOP, T))
    return {
        "xT": (n((K, T)) * s).astype(np.float32),
        "w1": (n((E, K, H)) / np.sqrt(K) / s[None]).astype(np.float32),
        "w3": (n((E, K, H)) / np.sqrt(K) / s[None] * u[None, None, :]).astype(np.float32),
        "w2": (n((E, H, N)) / np.sqrt(H) / u[None, :, None]).astype(np.float32),
        "gate": np.stack([np.tile(r, (N, 1)) for r in g]).astype(np.float32),
        "offs": striped(slot_token),
        "pos1": striped(pos[0]),
        "pos2": striped(pos[1]),
        "pos3": striped(pos[2]),
        "pos4": striped(pos[3]),
    }


def reference(xT, w1, w3, w2, gate, offs, pos1, pos2, pos3, pos4):
    idx = unstriped(offs)
    xq = mxq(f64(xT)[:, idx], 0, "e4m3")
    h = sigmoid(by_expert(mxq(f64(w1), 1, "e4m3"), xq))
    h = h * by_expert(mxq(f64(w3), 1, "e4m3"), xq)
    y = by_expert(mxq(f64(w2), 1, "e4m3"), mxq(h, 0, "e4m3"))
    y = np.concatenate([y, np.zeros((N, PAD))], axis=1)
    return sum(f64(gate[r]) * y[:, unstriped(p)] for r, p in enumerate((pos1, pos2, pos3, pos4)))

@@ -1,0 +1,298 @@
+from contextlib import ExitStack
+
+import concourse.mybir as mybir
+from concourse.masks import make_identity
+
+K, T, E, C, H, N = 512, 1024, 8, 128, 512, 256
+TOP = 4
+PAD = 64
+SLOTS = E * C
+
+FLOPS = 2 * SLOTS * (2 * K * H + H * N)
+BYTES = 4 * (K * T + 2 * E * K * H + E * H * N + TOP * T + N * T) + 5 * 2 * 128 * 64
+
+F32 = mybir.dt.float32
+BF16 = mybir.dt.bfloat16
+U32 = mybir.dt.uint32
+U16 = mybir.dt.uint16
+U8 = mybir.dt.uint8
+FP8X4 = mybir.dt.float8_e4m3fn_x4
+SIGMOID = mybir.ActivationFunctionType.Sigmoid
+COPY = mybir.ActivationFunctionType.Copy
+MULT = mybir.AluOpType.mult
+
+P = 128
+PACK = 4
+LIST = 16
+ROW_BLOCKS = N // P
+X_PIECE = 512
+X_ON_SCALAR = 192
+W2_ON_SCALAR = 128
+GATHER = 256
+W2_EARLY = 0
+W2_LAG = 3
+TOKEN_BANKS = 3
+WEIGHTED_BUFS = 3
+BANK_EXPERTS = 4
+CHUNKS = ((0, 512), (512, 256), (768, 256))
+
+
+def tile_moe_ecr_glu_sigmoid_kernel(
+    tc, xT, w1, w3, w2, gate, offs, pos1, pos2, pos3, pos4, out
+):
+    nc = tc.nc
+
+    with ExitStack() as ctx:
+        keep = ctx.enter_context(tc.tile_pool(name="keep", bufs=1))
+        raw_pool = ctx.enter_context(tc.tile_pool(name="raw", bufs=15))
+        work = ctx.enter_context(tc.tile_pool(name="work", bufs=4))
+
+        def load_list(src, name):
+            tile = keep.tile([P, T // LIST], U16, name=name)
+            nc.sync.dma_start(tile[:], src)
+            return tile
+
+        def load_rows(rows):
+            raw = raw_pool.tile([P, PACK, rows.shape[1]], F32, name="raw", align_bytes=64)
+            nc.sync.dma_start(out=raw[:], in_=rows.rearrange("(p j) w -> p j w", j=PACK))
+            return raw
+
+        def new_grouped(width):
+            return work.tile([P, width, PACK], BF16, name="grouped", bufs=3, align_bytes=64)
+
+        def interleave(grouped, raw, on_scalar):
+            width = raw.shape[2]
+            for engine_copy, lo, hi in ((nc.scalar.copy, 0, on_scalar), (nc.vector.tensor_copy, on_scalar, width)):
+                if hi > lo:
+                    engine_copy(
+                        out=grouped[:, lo:hi, :].rearrange("p (c i) j -> p c j i", i=4),
+                        in_=raw[:, :, lo:hi].rearrange("p j (c i) -> p c j i", i=4),
+                    )
+
+        def quantize(grouped, codes, scales):
+            nc.vector.quantize_mx(
+                out=codes.bitcast(FP8X4), scales=scales, in_=grouped[:].rearrange("p w j -> p (w j)")
+            )
+
+        def quantize_weight(grouped):
+            width = grouped.shape[1]
+            codes = work.tile([P, width], U32, name="w_codes", bufs=3, align_bytes=64)
+            scales = work.tile([P, width], U8, name="w_scales", bufs=3, align_bytes=64)
+            quantize(grouped, codes[:], scales[:])
+            return codes, scales
+
+        identity = keep.tile([P, P], F32)
+        make_identity(nc, identity[:])
+        x_codes = keep.tile([P, T], U32, align_bytes=64)
+        x_scales = keep.tile([P, T], U8, align_bytes=64)
+        nc.gpsimd.memset(x_scales[:], 0)
+        y = keep.tile([P, ROW_BLOCKS, SLOTS + PAD], F32)
+        nc.gpsimd.memset(y[:, :, SLOTS:], 0.0)
+        gate_rows = keep.tile([P, T], F32)
+        nc.gpsimd.memset(gate_rows[:], 0.0)
+
+        offsets = load_list(offs, "offsets")
+        x_raw = [load_rows(xT[:, t0 : t0 + X_PIECE]) for t0 in range(0, T, X_PIECE)]
+        nc.sync.dma_start(out=gate_rows[0:TOP, :], in_=gate[:, 0, :])
+        w1_raw, w3_raw, w2_raw, positions = [], [], [], []
+        for e in range(E):
+            w1_raw.append(load_rows(w1[e]))
+            w3_raw.append(load_rows(w3[e]))
+            if e < TOP:
+                positions.append(load_list((pos1, pos2, pos3, pos4)[e], "positions%d" % e))
+            if 0 <= e - W2_LAG < W2_EARLY:
+                w2_raw.append(load_rows(w2[e - W2_LAG]))
+        w2_raw.extend(load_rows(w2[e]) for e in range(W2_EARLY, E))
+
+        x_grouped = [new_grouped(X_PIECE) for raw in x_raw]
+        for grouped, raw in zip(x_grouped, x_raw):
+            interleave(grouped, raw, X_ON_SCALAR)
+        for i, grouped in enumerate(x_grouped):
+            cols = slice(i * X_PIECE, (i + 1) * X_PIECE)
+            quantize(grouped, x_codes[:, cols], x_scales[:, cols])
+        slot_codes, slot_scales = [], []
+
+        def gather_tokens(q):
+            entries = offsets[:, q * GATHER // LIST : (q + 1) * GATHER // LIST]
+            codes = keep.tile([P, GATHER], U32, name="slot_codes%d" % q, align_bytes=64)
+            scales = keep.tile([P, GATHER], U8, name="slot_scales%d" % q, align_bytes=64)
+            nc.vector.tensor_copy(codes[:], x_codes[:].indirect(entries))
+            nc.vector.tensor_copy(scales[:], x_scales[:].indirect(entries))
+            slot_codes.append(codes)
+            slot_scales.append(scales)
+
+        gate_cols = keep.tile([P, T // P, TOP], F32)
+
+        with tc.psum_pool(name="layers", bufs=2) as psum:
+            sums, turned = {}, {}
+
+            def first_products(e, codes, scales):
+                q, c0 = divmod(e * C, GATHER)
+                banks = []
+                for i, name in enumerate(("a_sum", "b_sum")):
+                    bank = psum.tile([C, H], F32, name=name)
+                    nc.tensor.matmul_mx(
+                        out=bank[:],
+                        lhsT=slot_codes[q][:, c0 : c0 + C].bitcast(FP8X4),
+                        lhsT_scale=slot_scales[q][:, c0 : c0 + C],
+                        rhs=codes[:, i * H : (i + 1) * H].bitcast(FP8X4),
+                        rhs_scale=scales[:, i * H : (i + 1) * H],
+                        start=True,
+                        stop=True,
+                    )
+                    banks.append(bank)
+                sums[e] = banks
+
+            def gate_values(e):
+                if e + 1 < E:
+                    sig = w1_raw[e + 1][:, 0, :]
+                else:
+                    sig = work.tile([C, H], F32, name="sig", bufs=1)[:]
+                nc.scalar.activation(sig, sums[e][0][:], SIGMOID)
+                if e + 1 < E:
+                    h = w3_raw[e + 1][:, 0, 0 : H // 2].bitcast(BF16)
+                else:
+                    h = work.tile([C, H], BF16, name="h", bufs=1)[:]
+                nc.vector.tensor_tensor(h, sums[e][1][:], sig, MULT)
+                words = h.bitcast(F32)
+                bank = psum.tile([P, 2, C], F32, name="turned")
+                for u in range(2):
+                    nc.tensor.transpose(bank[:, u, :], words[:, u : H // 2 : 2], identity[:])
+                sums[e] = bank
+
+            def pair_input(pair):
+                if pair not in pair_inputs:
+                    host = 2 * pair + 3
+                    if host < E:
+                        words = w1_raw[host][:, 1:3, :].rearrange("p j w -> p (j w)")
+                    else:
+                        words = work.tile([P, 2 * H], F32, name="last_pair", bufs=1, align_bytes=64)[:]
+                    pair_inputs[pair] = words
+                return pair_inputs[pair]
+
+            def hidden(e):
+                first = (2 + e % 2) * 2 * C
+                words = pair_input(e // 2)[:, first : first + 2 * C]
+                nc.scalar.copy(
+                    out=words.rearrange("p (c u) -> p c u", u=2),
+                    in_=sums[e][:].rearrange("p u c -> p c u"),
+                )
+                turned[e] = words
+
+            y_sums, pair_inputs, even_w2 = {}, {}, {}
+
+            def second_weights(e):
+                if e % 2 == 0:
+                    grouped = work.tile([P, N, PACK], BF16, name="w2_grouped", bufs=2, align_bytes=64)
+                    interleave(grouped, w2_raw[e], W2_ON_SCALAR)
+                    codes = work.tile([P, N], U32, name="w2_codes", bufs=2, align_bytes=64)
+                    scales = work.tile([P, N], U8, name="w2_scales", bufs=2, align_bytes=64)
+                    quantize(grouped, codes[:], scales[:])
+                    even_w2[e] = (codes, scales)
+                    return
+                grouped = pair_input(e // 2).bitcast(BF16).rearrange("p (w j) -> p w j", j=PACK)
+                interleave(grouped[:, 0:N, :], w2_raw[e], W2_ON_SCALAR)
+                codes = work.tile([P, N + 2 * C], U32, name="pair_codes", bufs=2, align_bytes=64)
+                scales = work.tile([P, N + 2 * C], U8, name="pair_scales", bufs=2, align_bytes=64)
+                quantize(grouped, codes[:], scales[:])
+                for nb in range(ROW_BLOCKS):
+                    for expert, (w_codes, w_scales) in ((e - 1, even_w2[e - 1]), (e, (codes, scales))):
+                        group, place = divmod(expert, BANK_EXPERTS)
+                        if place == 0:
+                            y_sums[nb] = psum.tile([P, BANK_EXPERTS * C], F32, name="y_sum%d" % nb, bufs=1)
+                        h0 = N + expert % 2 * C
+                        nc.tensor.matmul_mx(
+                            out=y_sums[nb][:, place * C : (place + 1) * C],
+                            lhsT=w_codes[:, nb * P : (nb + 1) * P].bitcast(FP8X4),
+                            lhsT_scale=w_scales[:, nb * P : (nb + 1) * P],
+                            rhs=codes[:, h0 : h0 + C].bitcast(FP8X4),
+                            rhs_scale=scales[:, h0 : h0 + C],
+                            start=True,
+                            stop=True,
+                        )
+                    if place == BANK_EXPERTS - 1:
+                        first = group * BANK_EXPERTS * C
+                        nc.scalar.copy(out=y[:, nb, first : first + BANK_EXPERTS * C], in_=y_sums[nb][:])
+
+            for half in range(2):
+                bank = psum.tile([P, 4, P], F32, name="y_sum%d" % half, bufs=1)
+                for b in range(4):
+                    t0 = (half * 4 + b) * P
+                    nc.tensor.transpose(bank[:, b, :], gate_rows[:, t0 : t0 + P], identity[:])
+                nc.scalar.copy(out=gate_cols[:, half * 4 : half * 4 + 4, :], in_=bank[:, :, 0:TOP])
+
+            for e in range(E + 2):
+                if e < E:
+                    if (e * C) % GATHER == 0:
+                        gather_tokens(e * C // GATHER)
+                    grouped = new_grouped(2 * H)
+                    interleave(grouped[:, 0:H, :], w1_raw[e], H)
+                    interleave(grouped[:, H : 2 * H, :], w3_raw[e], 0)
+                if 1 <= e <= E:
+                    gate_values(e - 1)
+                if e >= E:
+                    hidden(e - 2)
+                elif e >= 3 and e % 2 == 1:
+                    hidden(e - 3)
+                    hidden(e - 2)
+                if e < E:
+                    first_products(e, *quantize_weight(grouped))
+                if 0 <= e - W2_LAG < W2_EARLY:
+                    second_weights(e - W2_LAG)
+            for e in range(W2_EARLY, E):
+                second_weights(e)
+
+        with tc.psum_pool(name="combine", bufs=2) as psum:
+            steps = [(t0, width, r) for t0, width in CHUNKS for r in range(TOP)]
+            scaled, totals = {}, {}
+
+            def fetch(i):
+                t0, width, r = steps[i]
+                picked = raw_pool.tile([P, ROW_BLOCKS, width], F32, name="raw", align_bytes=64)
+                entries = positions[r][:, t0 // LIST : (t0 + width) // LIST]
+                for nb in range(ROW_BLOCKS):
+                    nc.vector.tensor_copy(picked[:, nb, :], y[:, nb, :].indirect(entries))
+                weighted = work.tile([P, width // P, N], F32, name="weighted", bufs=WEIGHTED_BUFS)
+                for pair in range(width // (2 * P)):
+                    bank = psum.tile([P, 2, ROW_BLOCKS, P], F32, name="by_token", bufs=TOKEN_BANKS)
+                    for b in range(2):
+                        for nb in range(ROW_BLOCKS):
+                            c0 = (2 * pair + b) * P
+                            nc.tensor.transpose(bank[:, b, nb, :], picked[:, nb, c0 : c0 + P], identity[:])
+                    for b in range(2):
+                        tb = t0 // P + 2 * pair + b
+                        nc.scalar.activation(
+                            weighted[:, 2 * pair + b, :],
+                            bank[:, b, :, :].rearrange("p a n -> p (a n)"),
+                            COPY,
+                            scale=gate_cols[:, tb, r : r + 1],
+                        )
+                scaled[i] = weighted
+
+            def add_up(i):
+                t0, width, r = steps[i]
+                if r == 0:
+                    totals[t0] = [psum.tile([P, width], F32, name="total%d" % nb) for nb in range(ROW_BLOCKS)]
+                blocks = width // P
+                for b in range(blocks):
+                    for nb in range(ROW_BLOCKS):
+                        nc.tensor.matmul(
+                            totals[t0][nb][:, b * P : (b + 1) * P],
+                            scaled[i][:, b, nb * P : (nb + 1) * P],
+                            identity[:],
+                            start=(r == 0 and b == 0),
+                            stop=(r == TOP - 1 and b == blocks - 1),
+                            is_transpose=True,
+                        )
+                if r == TOP - 1:
+                    for nb in range(ROW_BLOCKS):
+                        result = work.tile([P, width], F32, name="result")
+                        on_vector = nb == 1 and i == len(steps) - 1
+                        (nc.vector.tensor_copy if on_vector else nc.scalar.copy)(out=result[:], in_=totals[t0][nb][:])
+                        nc.sync.dma_start(out=out[nb * P : (nb + 1) * P, t0 : t0 + width], in_=result[:])
+
+            for i in range(len(steps) + 1):
+                if i < len(steps):
+                    fetch(i)
+                if i >= 1:
+                    add_up(i - 1)

@@ -8,9 +8,6 @@ TOP = 4
 PAD = 64
 SLOTS = E * C
 
-FLOPS = 2 * SLOTS * (2 * K * H + H * N)
-BYTES = 4 * (K * T + 2 * E * K * H + E * H * N + TOP * T + N * T) + 5 * 2 * 128 * 64
-
 F32 = mybir.dt.float32
 BF16 = mybir.dt.bfloat16
 U32 = mybir.dt.uint32
@@ -20,21 +17,29 @@ FP8X4 = mybir.dt.float8_e4m3fn_x4
 SIGMOID = mybir.ActivationFunctionType.Sigmoid
 COPY = mybir.ActivationFunctionType.Copy
 MULT = mybir.AluOpType.mult
+ADD = mybir.AluOpType.add
 
 P = 128
 PACK = 4
 LIST = 16
+BANK_BLOCKS = 4
 ROW_BLOCKS = N // P
+PAIRS = E // 2
+
 X_PIECE = 512
-X_ON_SCALAR = 192
-W2_ON_SCALAR = 128
 GATHER = 256
-W2_EARLY = 0
-W2_LAG = 3
-TOKEN_BANKS = 3
-WEIGHTED_BUFS = 3
-BANK_EXPERTS = 4
+X_ON_SCALAR = 192
+W2_ON_SCALAR = 160
 CHUNKS = ((0, 512), (512, 256), (768, 256))
+FUSED_FROM = 512
+
+LANDING_BUFS = 10
+PICKED_BUFS = 8
+WEIGHTED_BUFS = 3
+TOKEN_BANKS = 3
+
+FLOPS = 2 * SLOTS * (2 * K * H + H * N)
+BYTES = 4 * (K * T + 2 * E * K * H + E * H * N + TOP * T + N * T) + (1 + TOP) * 2 * P * (T // LIST)
 
 
 def tile_moe_ecr_glu_sigmoid_kernel(
@@ -42,257 +47,246 @@ def tile_moe_ecr_glu_sigmoid_kernel(
 ):
     nc = tc.nc
 
+    def interleave(grouped, raw, on_scalar):
+        shares = ((nc.scalar.copy, 0, on_scalar), (nc.vector.tensor_copy, on_scalar, raw.shape[2]))
+        for copy, lo, hi in shares:
+            if hi > lo:
+                copy(
+                    out=grouped[:, lo:hi, :].rearrange("p (c i) j -> p c j i", i=4),
+                    in_=raw[:, :, lo:hi].rearrange("p j (c i) -> p c j i", i=4),
+                )
+
+    def quantize(grouped, words, scales):
+        nc.vector.quantize_mx(
+            out=words.bitcast(FP8X4), scales=scales, in_=grouped.rearrange("p w j -> p (w j)")
+        )
+
+    def product(sums, stationary, moving):
+        nc.tensor.matmul_mx(
+            out=sums,
+            lhsT=stationary[0].bitcast(FP8X4),
+            lhsT_scale=stationary[1],
+            rhs=moving[0].bitcast(FP8X4),
+            rhs_scale=moving[1],
+            start=True,
+            stop=True,
+        )
+
+    def columns(operand, first, count):
+        return tuple(part[:, first : first + count] for part in operand)
+
     with ExitStack() as ctx:
         keep = ctx.enter_context(tc.tile_pool(name="keep", bufs=1))
-        raw_pool = ctx.enter_context(tc.tile_pool(name="raw", bufs=15))
-        work = ctx.enter_context(tc.tile_pool(name="work", bufs=4))
-
-        def load_list(src, name):
-            tile = keep.tile([P, T // LIST], U16, name=name)
-            nc.sync.dma_start(tile[:], src)
-            return tile
-
-        def load_rows(rows):
-            raw = raw_pool.tile([P, PACK, rows.shape[1]], F32, name="raw", align_bytes=64)
-            nc.sync.dma_start(out=raw[:], in_=rows.rearrange("(p j) w -> p j w", j=PACK))
-            return raw
-
-        def new_grouped(width):
-            return work.tile([P, width, PACK], BF16, name="grouped", bufs=3, align_bytes=64)
-
-        def interleave(grouped, raw, on_scalar):
-            width = raw.shape[2]
-            for engine_copy, lo, hi in ((nc.scalar.copy, 0, on_scalar), (nc.vector.tensor_copy, on_scalar, width)):
-                if hi > lo:
-                    engine_copy(
-                        out=grouped[:, lo:hi, :].rearrange("p (c i) j -> p c j i", i=4),
-                        in_=raw[:, :, lo:hi].rearrange("p j (c i) -> p c j i", i=4),
-                    )
-
-        def quantize(grouped, codes, scales):
-            nc.vector.quantize_mx(
-                out=codes.bitcast(FP8X4), scales=scales, in_=grouped[:].rearrange("p w j -> p (w j)")
-            )
-
-        def quantize_weight(grouped):
-            width = grouped.shape[1]
-            codes = work.tile([P, width], U32, name="w_codes", bufs=3, align_bytes=64)
-            scales = work.tile([P, width], U8, name="w_scales", bufs=3, align_bytes=64)
-            quantize(grouped, codes[:], scales[:])
-            return codes, scales
+        landing = ctx.enter_context(tc.tile_pool(name="landing", bufs=1))
 
         identity = keep.tile([P, P], F32)
         make_identity(nc, identity[:])
-        x_codes = keep.tile([P, T], U32, align_bytes=64)
-        x_scales = keep.tile([P, T], U8, align_bytes=64)
-        nc.gpsimd.memset(x_scales[:], 0)
-        y = keep.tile([P, ROW_BLOCKS, SLOTS + PAD], F32)
-        nc.gpsimd.memset(y[:, :, SLOTS:], 0.0)
+        token_words = keep.tile([P, T], U32, align_bytes=64)
+        token_scales = keep.tile([P, T], U8, align_bytes=64)
+        nc.gpsimd.memset(token_scales[:], 0)
+        y = [keep.tile([P, SLOTS + PAD], F32, name="y%d" % nb) for nb in range(ROW_BLOCKS)]
+        for rows in y:
+            nc.gpsimd.memset(rows[:, SLOTS:], 0.0)
         gate_rows = keep.tile([P, T], F32)
         nc.gpsimd.memset(gate_rows[:], 0.0)
-
-        offsets = load_list(offs, "offsets")
-        x_raw = [load_rows(xT[:, t0 : t0 + X_PIECE]) for t0 in range(0, T, X_PIECE)]
-        nc.sync.dma_start(out=gate_rows[0:TOP, :], in_=gate[:, 0, :])
-        w1_raw, w3_raw, w2_raw, positions = [], [], [], []
-        for e in range(E):
-            w1_raw.append(load_rows(w1[e]))
-            w3_raw.append(load_rows(w3[e]))
-            if e < TOP:
-                positions.append(load_list((pos1, pos2, pos3, pos4)[e], "positions%d" % e))
-            if 0 <= e - W2_LAG < W2_EARLY:
-                w2_raw.append(load_rows(w2[e - W2_LAG]))
-        w2_raw.extend(load_rows(w2[e]) for e in range(W2_EARLY, E))
-
-        x_grouped = [new_grouped(X_PIECE) for raw in x_raw]
-        for grouped, raw in zip(x_grouped, x_raw):
-            interleave(grouped, raw, X_ON_SCALAR)
-        for i, grouped in enumerate(x_grouped):
-            cols = slice(i * X_PIECE, (i + 1) * X_PIECE)
-            quantize(grouped, x_codes[:, cols], x_scales[:, cols])
-        slot_codes, slot_scales = [], []
-
-        def gather_tokens(q):
-            entries = offsets[:, q * GATHER // LIST : (q + 1) * GATHER // LIST]
-            codes = keep.tile([P, GATHER], U32, name="slot_codes%d" % q, align_bytes=64)
-            scales = keep.tile([P, GATHER], U8, name="slot_scales%d" % q, align_bytes=64)
-            nc.vector.tensor_copy(codes[:], x_codes[:].indirect(entries))
-            nc.vector.tensor_copy(scales[:], x_scales[:].indirect(entries))
-            slot_codes.append(codes)
-            slot_scales.append(scales)
-
         gate_cols = keep.tile([P, T // P, TOP], F32)
+        fused_gate = keep.tile([P, T - FUSED_FROM], F32)
 
-        with tc.psum_pool(name="layers", bufs=2) as psum:
-            sums, turned = {}, {}
+        def load_list(source, name):
+            tile = keep.tile([P, T // LIST], U16, name=name)
+            nc.sync.dma_start(tile[:], source)
+            return tile
 
-            def first_products(e, codes, scales):
-                q, c0 = divmod(e * C, GATHER)
-                banks = []
-                for i, name in enumerate(("a_sum", "b_sum")):
-                    bank = psum.tile([C, H], F32, name=name)
-                    nc.tensor.matmul_mx(
-                        out=bank[:],
-                        lhsT=slot_codes[q][:, c0 : c0 + C].bitcast(FP8X4),
-                        lhsT_scale=slot_scales[q][:, c0 : c0 + C],
-                        rhs=codes[:, i * H : (i + 1) * H].bitcast(FP8X4),
-                        rhs_scale=scales[:, i * H : (i + 1) * H],
-                        start=True,
-                        stop=True,
-                    )
-                    banks.append(bank)
-                sums[e] = banks
+        def load_rows(pool, rows, tag, bufs):
+            raw = pool.tile([P, PACK, rows.shape[1]], F32, name=tag, bufs=bufs, align_bytes=64)
+            nc.sync.dma_start(out=raw[:], in_=rows.rearrange("(p j) w -> p j w", j=PACK))
+            return raw
 
-            def gate_values(e):
+        with tc.tile_pool(name="layers", bufs=3) as work, tc.psum_pool(name="sums", bufs=2) as psum:
+
+            def new_operand(pool, width, tag, bufs):
+                words = pool.tile([P, width], U32, name=tag + "_words", bufs=bufs, align_bytes=64)
+                scales = pool.tile([P, width], U8, name=tag + "_scales", bufs=bufs, align_bytes=64)
+                return words[:], scales[:]
+
+            offsets = load_list(offs, "offsets")
+            x_raw = load_rows(work, xT, "x_raw", 1)
+            nc.sync.dma_start(out=gate_rows[0:TOP, :], in_=gate[:, 0, :])
+            w1_raw, w3_raw, positions = [], [], []
+            for e in range(E):
+                w1_raw.append(load_rows(landing, w1[e], "w13_raw", LANDING_BUFS))
+                w3_raw.append(load_rows(landing, w3[e], "w13_raw", LANDING_BUFS))
+                if e < TOP:
+                    positions.append(load_list((pos1, pos2, pos3, pos4)[e], "positions%d" % e))
+            w2_raw = [load_rows(landing, w2[e], "w2_raw", E) for e in range(E)]
+            nc.sync.dma_start(out=fused_gate[:], in_=gate[TOP - 1, 0:P, FUSED_FROM:T])
+
+            pieces = [slice(t0, t0 + X_PIECE) for t0 in range(0, T, X_PIECE)]
+            x_grouped = [work.tile([P, X_PIECE, PACK], BF16, name="grouped", align_bytes=64) for piece in pieces]
+            for piece, grouped in zip(pieces, x_grouped):
+                interleave(grouped, x_raw[:, :, piece], X_ON_SCALAR)
+            for piece, grouped in zip(pieces, x_grouped):
+                quantize(grouped[:], token_words[:, piece], token_scales[:, piece])
+
+            for half in range(2):
+                bank = psum.tile([P, BANK_BLOCKS, P], F32, name="y_sum%d" % half, bufs=1)
+                blocks = range(half * BANK_BLOCKS, (half + 1) * BANK_BLOCKS)
+                for b, block in enumerate(blocks):
+                    nc.tensor.transpose(bank[:, b, :], gate_rows[:, block * P : (block + 1) * P], identity[:])
+                nc.scalar.copy(out=gate_cols[:, blocks.start : blocks.stop, :], in_=bank[:, :, 0:TOP])
+
+            slot_operands, first_sums, turned, pair_inputs, even_w2, y_sums = [], {}, {}, {}, {}, {}
+
+            def gather_slots(first):
+                entries = offsets[:, first // LIST : (first + GATHER) // LIST]
+                words, scales = new_operand(keep, GATHER, "slots%d" % first, 1)
+                nc.vector.tensor_copy(words, token_words[:].indirect(entries))
+                nc.vector.tensor_copy(scales, token_scales[:].indirect(entries))
+                slot_operands.append((words, scales))
+
+            def first_layer(e, grouped):
+                weights = new_operand(work, 2 * H, "w13", 3)
+                quantize(grouped[:], *weights)
+                slots = columns(slot_operands[e * C // GATHER], e * C % GATHER, C)
+                first_sums[e] = [psum.tile([C, H], F32, name=tag) for tag in ("a_sum", "b_sum")]
+                for i, bank in enumerate(first_sums[e]):
+                    product(bank[:], slots, columns(weights, i * H, H))
+
+            def hidden(e):
                 if e + 1 < E:
                     sig = w1_raw[e + 1][:, 0, :]
+                    h_pairs = w3_raw[e + 1][:, 0, 0 : H // 2]
                 else:
-                    sig = work.tile([C, H], F32, name="sig", bufs=1)[:]
-                nc.scalar.activation(sig, sums[e][0][:], SIGMOID)
-                if e + 1 < E:
-                    h = w3_raw[e + 1][:, 0, 0 : H // 2].bitcast(BF16)
-                else:
-                    h = work.tile([C, H], BF16, name="h", bufs=1)[:]
-                nc.vector.tensor_tensor(h, sums[e][1][:], sig, MULT)
-                words = h.bitcast(F32)
-                bank = psum.tile([P, 2, C], F32, name="turned")
+                    sig = work.tile([C, H], F32, name="last_sig", bufs=1)[:]
+                    h_pairs = work.tile([C, H // 2], F32, name="last_h", bufs=1)[:]
+                a_sum, b_sum = first_sums[e]
+                nc.scalar.activation(sig, a_sum[:], SIGMOID)
+                nc.vector.tensor_tensor(h_pairs.bitcast(BF16), b_sum[:], sig, MULT)
+                turned[e] = psum.tile([P, 2, C], F32, name="turned")
                 for u in range(2):
-                    nc.tensor.transpose(bank[:, u, :], words[:, u : H // 2 : 2], identity[:])
-                sums[e] = bank
+                    nc.tensor.transpose(turned[e][:, u, :], h_pairs[:, u : H // 2 : 2], identity[:])
 
             def pair_input(pair):
                 if pair not in pair_inputs:
-                    host = 2 * pair + 3
-                    if host < E:
-                        words = w1_raw[host][:, 1:3, :].rearrange("p j w -> p (j w)")
+                    if 2 * pair + 3 < E:
+                        pair_inputs[pair] = w1_raw[2 * pair + 3][:, 1:3, :].rearrange("p j w -> p (j w)")
                     else:
-                        words = work.tile([P, 2 * H], F32, name="last_pair", bufs=1, align_bytes=64)[:]
-                    pair_inputs[pair] = words
+                        pair_inputs[pair] = work.tile([P, 2 * H], F32, name="last_pair", bufs=1, align_bytes=64)[:]
                 return pair_inputs[pair]
 
-            def hidden(e):
-                first = (2 + e % 2) * 2 * C
-                words = pair_input(e // 2)[:, first : first + 2 * C]
+            def place_hidden(e):
+                first = 2 * (N + e % 2 * C)
                 nc.scalar.copy(
-                    out=words.rearrange("p (c u) -> p c u", u=2),
-                    in_=sums[e][:].rearrange("p u c -> p c u"),
+                    out=pair_input(e // 2)[:, first : first + 2 * C].rearrange("p (c u) -> p c u", u=2),
+                    in_=turned[e][:].rearrange("p u c -> p c u"),
                 )
-                turned[e] = words
 
-            y_sums, pair_inputs, even_w2 = {}, {}, {}
-
-            def second_weights(e):
+            def second_layer(e):
                 if e % 2 == 0:
-                    grouped = work.tile([P, N, PACK], BF16, name="w2_grouped", bufs=2, align_bytes=64)
+                    grouped = work.tile([P, N, PACK], BF16, name="w2_grouped", align_bytes=64)
                     interleave(grouped, w2_raw[e], W2_ON_SCALAR)
-                    codes = work.tile([P, N], U32, name="w2_codes", bufs=2, align_bytes=64)
-                    scales = work.tile([P, N], U8, name="w2_scales", bufs=2, align_bytes=64)
-                    quantize(grouped, codes[:], scales[:])
-                    even_w2[e] = (codes, scales)
+                    even_w2[e] = new_operand(work, N, "w2", 2)
+                    quantize(grouped[:], *even_w2[e])
                     return
                 grouped = pair_input(e // 2).bitcast(BF16).rearrange("p (w j) -> p w j", j=PACK)
                 interleave(grouped[:, 0:N, :], w2_raw[e], W2_ON_SCALAR)
-                codes = work.tile([P, N + 2 * C], U32, name="pair_codes", bufs=2, align_bytes=64)
-                scales = work.tile([P, N + 2 * C], U8, name="pair_scales", bufs=2, align_bytes=64)
-                quantize(grouped, codes[:], scales[:])
+                pair = new_operand(work, N + 2 * C, "pair", 2)
+                quantize(grouped, *pair)
                 for nb in range(ROW_BLOCKS):
-                    for expert, (w_codes, w_scales) in ((e - 1, even_w2[e - 1]), (e, (codes, scales))):
-                        group, place = divmod(expert, BANK_EXPERTS)
-                        if place == 0:
-                            y_sums[nb] = psum.tile([P, BANK_EXPERTS * C], F32, name="y_sum%d" % nb, bufs=1)
-                        h0 = N + expert % 2 * C
-                        nc.tensor.matmul_mx(
-                            out=y_sums[nb][:, place * C : (place + 1) * C],
-                            lhsT=w_codes[:, nb * P : (nb + 1) * P].bitcast(FP8X4),
-                            lhsT_scale=w_scales[:, nb * P : (nb + 1) * P],
-                            rhs=codes[:, h0 : h0 + C].bitcast(FP8X4),
-                            rhs_scale=scales[:, h0 : h0 + C],
-                            start=True,
-                            stop=True,
+                    for odd, weights in enumerate((even_w2[e - 1], pair)):
+                        product(
+                            y_sums[nb, odd][:, e // 2, :], columns(weights, nb * P, P), columns(pair, N + odd * C, C)
                         )
-                    if place == BANK_EXPERTS - 1:
-                        first = group * BANK_EXPERTS * C
-                        nc.scalar.copy(out=y[:, nb, first : first + BANK_EXPERTS * C], in_=y_sums[nb][:])
 
-            for half in range(2):
-                bank = psum.tile([P, 4, P], F32, name="y_sum%d" % half, bufs=1)
-                for b in range(4):
-                    t0 = (half * 4 + b) * P
-                    nc.tensor.transpose(bank[:, b, :], gate_rows[:, t0 : t0 + P], identity[:])
-                nc.scalar.copy(out=gate_cols[:, half * 4 : half * 4 + 4, :], in_=bank[:, :, 0:TOP])
-
-            for e in range(E + 2):
+            for e in range(E + 1):
                 if e < E:
-                    if (e * C) % GATHER == 0:
-                        gather_tokens(e * C // GATHER)
-                    grouped = new_grouped(2 * H)
+                    if e * C % GATHER == 0:
+                        gather_slots(e * C)
+                    grouped = work.tile([P, 2 * H, PACK], BF16, name="grouped", align_bytes=64)
                     interleave(grouped[:, 0:H, :], w1_raw[e], H)
                     interleave(grouped[:, H : 2 * H, :], w3_raw[e], 0)
-                if 1 <= e <= E:
-                    gate_values(e - 1)
-                if e >= E:
-                    hidden(e - 2)
-                elif e >= 3 and e % 2 == 1:
-                    hidden(e - 3)
-                    hidden(e - 2)
+                if e >= 1:
+                    hidden(e - 1)
+                if e >= 3 and e % 2 == 1:
+                    place_hidden(e - 3)
+                    place_hidden(e - 2)
                 if e < E:
-                    first_products(e, *quantize_weight(grouped))
-                if 0 <= e - W2_LAG < W2_EARLY:
-                    second_weights(e - W2_LAG)
-            for e in range(W2_EARLY, E):
-                second_weights(e)
+                    first_layer(e, grouped)
+            place_hidden(E - 2)
+            place_hidden(E - 1)
 
-        with tc.psum_pool(name="combine", bufs=2) as psum:
-            steps = [(t0, width, r) for t0, width in CHUNKS for r in range(TOP)]
-            scaled, totals = {}, {}
+            for odd in range(2):
+                y_sums[0, odd] = psum.tile([P, PAIRS, C], F32, name="y_sum%d" % odd, bufs=1)
+                y_sums[1, odd] = psum.tile([P, PAIRS, C], F32, name=("a_sum", "b_sum")[odd])
+            for e in range(E):
+                second_layer(e)
+            for nb in range(ROW_BLOCKS):
+                slots = y[nb][:, 0:SLOTS].rearrange("p (pair odd c) -> p odd pair c", odd=2, c=C)
+                for odd in range(2):
+                    copy = nc.vector.tensor_copy if (nb, odd) == (0, 0) else nc.scalar.copy
+                    copy(out=slots[:, odd, :, :], in_=y_sums[nb, odd][:])
 
-            def fetch(i):
-                t0, width, r = steps[i]
-                picked = raw_pool.tile([P, ROW_BLOCKS, width], F32, name="raw", align_bytes=64)
+        with tc.tile_pool(name="combine", bufs=4) as work, tc.psum_pool(name="turns", bufs=2) as psum:
+            steps = []
+            for t0, width in CHUNKS:
+                for row_blocks in ((0,), (1,)) if t0 == 0 else ((0, 1),):
+                    steps.extend((t0, width, r, row_blocks) for r in range(TOP))
+            products, totals = {}, {}
+
+            def fetch(step):
+                t0, width, r, row_blocks = step
                 entries = positions[r][:, t0 // LIST : (t0 + width) // LIST]
-                for nb in range(ROW_BLOCKS):
-                    nc.vector.tensor_copy(picked[:, nb, :], y[:, nb, :].indirect(entries))
-                weighted = work.tile([P, width // P, N], F32, name="weighted", bufs=WEIGHTED_BUFS)
-                for pair in range(width // (2 * P)):
-                    bank = psum.tile([P, 2, ROW_BLOCKS, P], F32, name="by_token", bufs=TOKEN_BANKS)
-                    for b in range(2):
-                        for nb in range(ROW_BLOCKS):
-                            c0 = (2 * pair + b) * P
-                            nc.tensor.transpose(bank[:, b, nb, :], picked[:, nb, c0 : c0 + P], identity[:])
-                    for b in range(2):
-                        tb = t0 // P + 2 * pair + b
-                        nc.scalar.activation(
-                            weighted[:, 2 * pair + b, :],
-                            bank[:, b, :, :].rearrange("p a n -> p (a n)"),
-                            COPY,
-                            scale=gate_cols[:, tb, r : r + 1],
-                        )
-                scaled[i] = weighted
+                picked = [work.tile([P, width], F32, name="picked", bufs=PICKED_BUFS) for nb in row_blocks]
+                if r == TOP - 1 and t0 >= FUSED_FROM:
+                    weights = fused_gate[:, t0 - FUSED_FROM : t0 - FUSED_FROM + width]
+                    for nb, tile in zip(row_blocks, picked):
+                        nc.vector.tensor_tensor(tile[:], y[nb][:].indirect(entries), weights, MULT)
+                    products[step] = picked
+                    return
+                for nb, tile in zip(row_blocks, picked):
+                    nc.vector.tensor_copy(tile[:], y[nb][:].indirect(entries))
+                bank = psum.tile([P, width // P, len(row_blocks), P], F32, name="by_token", bufs=TOKEN_BANKS)
+                for i, tile in enumerate(picked):
+                    for b in range(width // P):
+                        nc.tensor.transpose(bank[:, b, i, :], tile[:, b * P : (b + 1) * P], identity[:])
+                weighted = work.tile([P, width // P, len(row_blocks), P], F32, name="weighted", bufs=WEIGHTED_BUFS)
+                for b in range(width // P):
+                    nc.scalar.activation(
+                        weighted[:, b, :, :].rearrange("p i n -> p (i n)"),
+                        bank[:, b, :, :].rearrange("p i n -> p (i n)"),
+                        COPY,
+                        scale=gate_cols[:, t0 // P + b, r : r + 1],
+                    )
+                products[step] = weighted
 
-            def add_up(i):
-                t0, width, r = steps[i]
+            def add_up(step):
+                t0, width, r, row_blocks = step
+                turned_lists = TOP - 1 if t0 >= FUSED_FROM else TOP
                 if r == 0:
-                    totals[t0] = [psum.tile([P, width], F32, name="total%d" % nb) for nb in range(ROW_BLOCKS)]
-                blocks = width // P
-                for b in range(blocks):
-                    for nb in range(ROW_BLOCKS):
-                        nc.tensor.matmul(
-                            totals[t0][nb][:, b * P : (b + 1) * P],
-                            scaled[i][:, b, nb * P : (nb + 1) * P],
-                            identity[:],
-                            start=(r == 0 and b == 0),
-                            stop=(r == TOP - 1 and b == blocks - 1),
-                            is_transpose=True,
-                        )
+                    for nb in row_blocks:
+                        totals[nb] = psum.tile([P, width], F32, name="total%d" % nb)
+                if r < turned_lists:
+                    for b in range(width // P):
+                        for i, nb in enumerate(row_blocks):
+                            nc.tensor.matmul(
+                                totals[nb][:, b * P : (b + 1) * P],
+                                products[step][:, b, i, :],
+                                identity[:],
+                                start=(r == 0 and b == 0),
+                                stop=(r == turned_lists - 1 and b == width // P - 1),
+                                is_transpose=True,
+                            )
                 if r == TOP - 1:
-                    for nb in range(ROW_BLOCKS):
+                    for i, nb in enumerate(row_blocks):
                         result = work.tile([P, width], F32, name="result")
-                        on_vector = nb == 1 and i == len(steps) - 1
-                        (nc.vector.tensor_copy if on_vector else nc.scalar.copy)(out=result[:], in_=totals[t0][nb][:])
+                        if r < turned_lists:
+                            nc.scalar.copy(out=result[:], in_=totals[nb][:])
+                        else:
+                            nc.vector.tensor_tensor(result[:], totals[nb][:], products[step][i][:], ADD)
                         nc.sync.dma_start(out=out[nb * P : (nb + 1) * P, t0 : t0 + width], in_=result[:])
 
             for i in range(len(steps) + 1):
                 if i < len(steps):
-                    fetch(i)
+                    fetch(steps[i])
                 if i >= 1:
-                    add_up(i - 1)
+                    add_up(steps[i - 1])

@@ -22,7 +22,6 @@ ADD = mybir.AluOpType.add
 P = 128
 PACK = 4
 LIST = 16
-BANK_BLOCKS = 4
 ROW_BLOCKS = N // P
 PAIRS = E // 2
 
@@ -30,6 +29,8 @@ X_PIECE = 512
 GATHER = 256
 X_ON_SCALAR = 192
 W2_ON_SCALAR = 160
+LAST_W2_ON_SCALAR = 96
+LAST_H_HOST = 2
 CHUNKS = ((0, 512), (512, 256), (768, 256))
 FUSED_FROM = 512
 
@@ -87,9 +88,9 @@ def tile_moe_ecr_glu_sigmoid_kernel(
         y = [keep.tile([P, SLOTS + PAD], F32, name="y%d" % nb) for nb in range(ROW_BLOCKS)]
         for rows in y:
             nc.gpsimd.memset(rows[:, SLOTS:], 0.0)
-        gate_rows = keep.tile([P, T], F32)
+        gate_rows = keep.tile([P, P], F32)
         nc.gpsimd.memset(gate_rows[:], 0.0)
-        gate_cols = keep.tile([P, T // P, TOP], F32)
+        gate_cols = keep.tile([P, TOP, T // P], F32)
         fused_gate = keep.tile([P, T - FUSED_FROM], F32)
 
         def load_list(source, name):
@@ -109,9 +110,8 @@ def tile_moe_ecr_glu_sigmoid_kernel(
                 scales = pool.tile([P, width], U8, name=tag + "_scales", bufs=bufs, align_bytes=64)
                 return words[:], scales[:]
 
-            offsets = load_list(offs, "offsets")
             x_raw = load_rows(work, xT, "x_raw", 1)
-            nc.sync.dma_start(out=gate_rows[0:TOP, :], in_=gate[:, 0, :])
+            offsets = load_list(offs, "offsets")
             w1_raw, w3_raw, positions = [], [], []
             for e in range(E):
                 w1_raw.append(load_rows(landing, w1[e], "w13_raw", LANDING_BUFS))
@@ -119,6 +119,9 @@ def tile_moe_ecr_glu_sigmoid_kernel(
                 if e < TOP:
                     positions.append(load_list((pos1, pos2, pos3, pos4)[e], "positions%d" % e))
             w2_raw = [load_rows(landing, w2[e], "w2_raw", E) for e in range(E)]
+            for r in range(TOP):
+                rows = gate_rows[r * (T // P) : (r + 1) * (T // P), :]
+                nc.sync.dma_start(out=rows, in_=gate[r, 0, :].rearrange("(b t) -> b t", t=P))
             nc.sync.dma_start(out=fused_gate[:], in_=gate[TOP - 1, 0:P, FUSED_FROM:T])
 
             pieces = [slice(t0, t0 + X_PIECE) for t0 in range(0, T, X_PIECE)]
@@ -128,14 +131,7 @@ def tile_moe_ecr_glu_sigmoid_kernel(
             for piece, grouped in zip(pieces, x_grouped):
                 quantize(grouped[:], token_words[:, piece], token_scales[:, piece])
 
-            for half in range(2):
-                bank = psum.tile([P, BANK_BLOCKS, P], F32, name="y_sum%d" % half, bufs=1)
-                blocks = range(half * BANK_BLOCKS, (half + 1) * BANK_BLOCKS)
-                for b, block in enumerate(blocks):
-                    nc.tensor.transpose(bank[:, b, :], gate_rows[:, block * P : (block + 1) * P], identity[:])
-                nc.scalar.copy(out=gate_cols[:, blocks.start : blocks.stop, :], in_=bank[:, :, 0:TOP])
-
-            slot_operands, first_sums, turned, pair_inputs, even_w2, y_sums = [], {}, {}, {}, {}, {}
+            slot_operands, first_sums, turned, pair_inputs, pairs, y_sums = [], {}, {}, {}, {}, {}
 
             def gather_slots(first):
                 entries = offsets[:, first // LIST : (first + GATHER) // LIST]
@@ -158,7 +154,7 @@ def tile_moe_ecr_glu_sigmoid_kernel(
                     h_pairs = w3_raw[e + 1][:, 0, 0 : H // 2]
                 else:
                     sig = work.tile([C, H], F32, name="last_sig", bufs=1)[:]
-                    h_pairs = work.tile([C, H // 2], F32, name="last_h", bufs=1)[:]
+                    h_pairs = w2_raw[LAST_H_HOST][:, 0, :]
                 a_sum, b_sum = first_sums[e]
                 nc.scalar.activation(sig, a_sum[:], SIGMOID)
                 nc.vector.tensor_tensor(h_pairs.bitcast(BF16), b_sum[:], sig, MULT)
@@ -182,51 +178,55 @@ def tile_moe_ecr_glu_sigmoid_kernel(
                 )
 
             def second_layer(e):
+                on_scalar = W2_ON_SCALAR if e < E - 1 else LAST_W2_ON_SCALAR
                 if e % 2 == 0:
-                    grouped = work.tile([P, N, PACK], BF16, name="w2_grouped", align_bytes=64)
-                    interleave(grouped, w2_raw[e], W2_ON_SCALAR)
-                    even_w2[e] = new_operand(work, N, "w2", 2)
-                    quantize(grouped[:], *even_w2[e])
-                    return
-                grouped = pair_input(e // 2).bitcast(BF16).rearrange("p (w j) -> p w j", j=PACK)
-                interleave(grouped[:, 0:N, :], w2_raw[e], W2_ON_SCALAR)
-                pair = new_operand(work, N + 2 * C, "pair", 2)
-                quantize(grouped, *pair)
+                    grouped = pair_input(e // 2).bitcast(BF16).rearrange("p (w j) -> p w j", j=PACK)
+                    interleave(grouped[:, 0:N, :], w2_raw[e], on_scalar)
+                    weights = pairs[e // 2] = new_operand(work, N + 2 * C, "pair", 2)
+                else:
+                    grouped = work.tile([P, N, PACK], BF16, name="w2_grouped", align_bytes=64)[:]
+                    interleave(grouped, w2_raw[e], on_scalar)
+                    weights = new_operand(work, N, "w2", 2)
+                quantize(grouped, *weights)
                 for nb in range(ROW_BLOCKS):
-                    for odd, weights in enumerate((even_w2[e - 1], pair)):
-                        product(
-                            y_sums[nb, odd][:, e // 2, :], columns(weights, nb * P, P), columns(pair, N + odd * C, C)
-                        )
+                    sums = last_sum[:] if (e, nb) == (E - 1, 0) else y_sums[nb, e % 2][:, e // 2, :]
+                    product(sums, columns(weights, nb * P, P), columns(pairs[e // 2], N + e % 2 * C, C))
 
-            for e in range(E + 1):
-                if e < E:
-                    if e * C % GATHER == 0:
-                        gather_slots(e * C)
-                    grouped = work.tile([P, 2 * H, PACK], BF16, name="grouped", align_bytes=64)
-                    interleave(grouped[:, 0:H, :], w1_raw[e], H)
-                    interleave(grouped[:, H : 2 * H, :], w3_raw[e], 0)
+            for e in range(E):
+                if e * C % GATHER == 0:
+                    gather_slots(e * C)
+                grouped = work.tile([P, 2 * H, PACK], BF16, name="grouped", align_bytes=64)
+                interleave(grouped[:, 0:H, :], w1_raw[e], H)
+                interleave(grouped[:, H : 2 * H, :], w3_raw[e], 0)
                 if e >= 1:
                     hidden(e - 1)
                 if e >= 3 and e % 2 == 1:
                     place_hidden(e - 3)
                     place_hidden(e - 2)
-                if e < E:
-                    first_layer(e, grouped)
+                first_layer(e, grouped)
             place_hidden(E - 2)
-            place_hidden(E - 1)
 
             for odd in range(2):
-                y_sums[0, odd] = psum.tile([P, PAIRS, C], F32, name="y_sum%d" % odd, bufs=1)
+                y_sums[0, odd] = psum.tile([P, PAIRS - odd, C], F32, name="y_sum%d" % odd, bufs=1)
                 y_sums[1, odd] = psum.tile([P, PAIRS, C], F32, name=("a_sum", "b_sum")[odd])
+            last_sum = psum.tile([P, C], F32, name="turned")
             for e in range(E):
                 second_layer(e)
-            for nb in range(ROW_BLOCKS):
-                slots = y[nb][:, 0:SLOTS].rearrange("p (pair odd c) -> p odd pair c", odd=2, c=C)
-                for odd in range(2):
-                    copy = nc.vector.tensor_copy if (nb, odd) == (0, 0) else nc.scalar.copy
-                    copy(out=slots[:, odd, :, :], in_=y_sums[nb, odd][:])
+                if e == LAST_H_HOST:
+                    hidden(E - 1)
+                    place_hidden(E - 1)
+            by_expert = [rows[:, 0:SLOTS].rearrange("p (pair odd c) -> p odd pair c", odd=2, c=C) for rows in y]
+            nc.scalar.copy(out=by_expert[0][:, 1, 0 : PAIRS - 1, :], in_=y_sums[0, 1][:])
+            nc.scalar.copy(out=by_expert[0][:, 0, :, :], in_=y_sums[0, 0][:])
+            nc.vector.tensor_copy(out=y[0][:, SLOTS - C : SLOTS], in_=last_sum[:])
+            for odd in range(2):
+                nc.scalar.copy(out=by_expert[1][:, odd, :, :], in_=y_sums[1, odd][:])
 
         with tc.tile_pool(name="combine", bufs=4) as work, tc.psum_pool(name="turns", bufs=2) as psum:
+            gate_turned = psum.tile([P, P], F32, bufs=1)
+            nc.tensor.transpose(gate_turned[:], gate_rows[:], identity[:])
+            nc.scalar.copy(out=gate_cols[:].rearrange("p r b -> p (r b)"), in_=gate_turned[:, 0 : TOP * T // P])
+
             steps = []
             for t0, width in CHUNKS:
                 for row_blocks in ((0,), (1,)) if t0 == 0 else ((0, 1),):
@@ -255,7 +255,7 @@ def tile_moe_ecr_glu_sigmoid_kernel(
                         weighted[:, b, :, :].rearrange("p i n -> p (i n)"),
                         bank[:, b, :, :].rearrange("p i n -> p (i n)"),
                         COPY,
-                        scale=gate_cols[:, t0 // P + b, r : r + 1],
+                        scale=gate_cols[:, r, t0 // P + b : t0 // P + b + 1],
                     )
                 products[step] = weighted
 

@@ -15,7 +15,6 @@ U16 = mybir.dt.uint16
 U8 = mybir.dt.uint8
 FP8X4 = mybir.dt.float8_e4m3fn_x4
 SIGMOID = mybir.ActivationFunctionType.Sigmoid
-COPY = mybir.ActivationFunctionType.Copy
 MULT = mybir.AluOpType.mult
 ADD = mybir.AluOpType.add
 
@@ -32,12 +31,11 @@ W2_ON_SCALAR = 160
 LAST_W2_ON_SCALAR = 96
 LAST_H_HOST = 2
 CHUNKS = ((0, 512), (512, 256), (768, 256))
-FUSED_FROM = 512
+FUSED_FROM = 768
 
 LANDING_BUFS = 10
-PICKED_BUFS = 8
-WEIGHTED_BUFS = 3
-TOKEN_BANKS = 3
+PICKED_BUFS = 4
+TOKEN_BANKS = 4
 
 FLOPS = 2 * SLOTS * (2 * K * H + H * N)
 BYTES = 4 * (K * T + 2 * E * K * H + E * H * N + TOP * T + N * T) + (1 + TOP) * 2 * P * (T // LIST)
@@ -88,10 +86,7 @@ def tile_moe_ecr_glu_sigmoid_kernel(
         y = [keep.tile([P, SLOTS + PAD], F32, name="y%d" % nb) for nb in range(ROW_BLOCKS)]
         for rows in y:
             nc.gpsimd.memset(rows[:, SLOTS:], 0.0)
-        gate_rows = keep.tile([P, P], F32)
-        nc.gpsimd.memset(gate_rows[:], 0.0)
-        gate_cols = keep.tile([P, TOP, T // P], F32)
-        fused_gate = keep.tile([P, T - FUSED_FROM], F32)
+        gates = {t0: keep.tile([P, TOP, width], F32, name="gate%d" % t0) for t0, width in CHUNKS}
 
         def load_list(source, name):
             tile = keep.tile([P, T // LIST], U16, name=name)
@@ -119,10 +114,10 @@ def tile_moe_ecr_glu_sigmoid_kernel(
                 if e < TOP:
                     positions.append(load_list((pos1, pos2, pos3, pos4)[e], "positions%d" % e))
             w2_raw = [load_rows(landing, w2[e], "w2_raw", E) for e in range(E)]
-            for r in range(TOP):
-                rows = gate_rows[r * (T // P) : (r + 1) * (T // P), :]
-                nc.sync.dma_start(out=rows, in_=gate[r, 0, :].rearrange("(b t) -> b t", t=P))
-            nc.sync.dma_start(out=fused_gate[:], in_=gate[TOP - 1, 0:P, FUSED_FROM:T])
+            for t0, width in CHUNKS:
+                for r in range(0, TOP, 2):
+                    rows = gate[r : r + 2, 0:P, t0 : t0 + width].rearrange("r p t -> p r t")
+                    nc.sync.dma_start(out=gates[t0][:, r : r + 2, :], in_=rows)
 
             pieces = [slice(t0, t0 + X_PIECE) for t0 in range(0, T, X_PIECE)]
             x_grouped = [work.tile([P, X_PIECE, PACK], BF16, name="grouped", align_bytes=64) for piece in pieces]
@@ -223,70 +218,46 @@ def tile_moe_ecr_glu_sigmoid_kernel(
                 nc.scalar.copy(out=by_expert[1][:, odd, :, :], in_=y_sums[1, odd][:])
 
         with tc.tile_pool(name="combine", bufs=4) as work, tc.psum_pool(name="turns", bufs=2) as psum:
-            gate_turned = psum.tile([P, P], F32, bufs=1)
-            nc.tensor.transpose(gate_turned[:], gate_rows[:], identity[:])
-            nc.scalar.copy(out=gate_cols[:].rearrange("p r b -> p (r b)"), in_=gate_turned[:, 0 : TOP * T // P])
-
             steps = []
             for t0, width in CHUNKS:
-                for row_blocks in ((0,), (1,)) if t0 == 0 else ((0, 1),):
-                    steps.extend((t0, width, r, row_blocks) for r in range(TOP))
-            products, totals = {}, {}
+                order = [(r, nb) for r in range(TOP) for nb in range(ROW_BLOCKS)]
+                if t0 == 0:
+                    order = [(r, nb) for nb in range(ROW_BLOCKS) for r in range(TOP)]
+                steps.extend((t0, width, r, nb) for r, nb in order)
+            by_token, by_row, fourth = {}, {}, {}
 
-            def fetch(step):
-                t0, width, r, row_blocks = step
-                entries = positions[r][:, t0 // LIST : (t0 + width) // LIST]
-                picked = [work.tile([P, width], F32, name="picked", bufs=PICKED_BUFS) for nb in row_blocks]
-                if r == TOP - 1 and t0 >= FUSED_FROM:
-                    weights = fused_gate[:, t0 - FUSED_FROM : t0 - FUSED_FROM + width]
-                    for nb, tile in zip(row_blocks, picked):
-                        nc.vector.tensor_tensor(tile[:], y[nb][:].indirect(entries), weights, MULT)
-                    products[step] = picked
-                    return
-                for nb, tile in zip(row_blocks, picked):
-                    nc.vector.tensor_copy(tile[:], y[nb][:].indirect(entries))
-                bank = psum.tile([P, width // P, len(row_blocks), P], F32, name="by_token", bufs=TOKEN_BANKS)
-                for i, tile in enumerate(picked):
-                    for b in range(width // P):
-                        nc.tensor.transpose(bank[:, b, i, :], tile[:, b * P : (b + 1) * P], identity[:])
-                weighted = work.tile([P, width // P, len(row_blocks), P], F32, name="weighted", bufs=WEIGHTED_BUFS)
-                for b in range(width // P):
-                    nc.scalar.activation(
-                        weighted[:, b, :, :].rearrange("p i n -> p (i n)"),
-                        bank[:, b, :, :].rearrange("p i n -> p (i n)"),
-                        COPY,
-                        scale=gate_cols[:, r, t0 // P + b : t0 // P + b + 1],
-                    )
-                products[step] = weighted
-
-            def add_up(step):
-                t0, width, r, row_blocks = step
+            for t0, width, r, nb in steps:
+                blocks = [slice(b, b + P) for b in range(0, width, P)]
                 turned_lists = TOP - 1 if t0 >= FUSED_FROM else TOP
+                entries = positions[r][:, t0 // LIST : (t0 + width) // LIST]
+                picked = work.tile([P, width], F32, name="picked", bufs=PICKED_BUFS)
+                nc.vector.tensor_tensor(picked[:], y[nb][:].indirect(entries), gates[t0][:, r, :], MULT)
                 if r == 0:
-                    for nb in row_blocks:
-                        totals[nb] = psum.tile([P, width], F32, name="total%d" % nb)
+                    by_token[nb] = psum.tile([P, width], F32, name="by_token", bufs=TOKEN_BANKS)
                 if r < turned_lists:
-                    for b in range(width // P):
-                        for i, nb in enumerate(row_blocks):
-                            nc.tensor.matmul(
-                                totals[nb][:, b * P : (b + 1) * P],
-                                products[step][:, b, i, :],
-                                identity[:],
-                                start=(r == 0 and b == 0),
-                                stop=(r == turned_lists - 1 and b == width // P - 1),
-                                is_transpose=True,
-                            )
-                if r == TOP - 1:
-                    for i, nb in enumerate(row_blocks):
+                    for block in blocks:
+                        nc.tensor.matmul(
+                            by_token[nb][:, block],
+                            picked[:, block],
+                            identity[:],
+                            start=(r == 0 and block == blocks[0]),
+                            stop=(r == turned_lists - 1 and block == blocks[-1]),
+                            is_transpose=True,
+                        )
+                if r == turned_lists - 1:
+                    summed = work.tile([P, width], F32, name="summed")
+                    nc.scalar.copy(out=summed[:], in_=by_token[nb][:])
+                    by_row[nb] = psum.tile([P, width], F32, name="by_row", bufs=4)
+                    for block in blocks:
+                        nc.tensor.transpose(by_row[nb][:, block], summed[:, block], identity[:])
+                if r == TOP - 1 and r < turned_lists:
+                    result = work.tile([P, width], F32, name="result")
+                    nc.scalar.copy(out=result[:], in_=by_row[nb][:])
+                    nc.sync.dma_start(out=out[nb * P : (nb + 1) * P, t0 : t0 + width], in_=result[:])
+                if r == turned_lists:
+                    fourth[nb] = picked
+                if r == turned_lists and nb == ROW_BLOCKS - 1:
+                    for rb in range(ROW_BLOCKS):
                         result = work.tile([P, width], F32, name="result")
-                        if r < turned_lists:
-                            nc.scalar.copy(out=result[:], in_=totals[nb][:])
-                        else:
-                            nc.vector.tensor_tensor(result[:], totals[nb][:], products[step][i][:], ADD)
-                        nc.sync.dma_start(out=out[nb * P : (nb + 1) * P, t0 : t0 + width], in_=result[:])
-
-            for i in range(len(steps) + 1):
-                if i < len(steps):
-                    fetch(steps[i])
-                if i >= 1:
-                    add_up(steps[i - 1])
+                        nc.vector.tensor_tensor(result[:], by_row[rb][:], fourth[rb][:], ADD)
+                        nc.sync.dma_start(out=out[rb * P : (rb + 1) * P, t0 : t0 + width], in_=result[:])

@@ -31,11 +31,11 @@ W2_ON_SCALAR = 160
 LAST_W2_ON_SCALAR = 96
 LAST_H_HOST = 2
 CHUNKS = ((0, 512), (512, 256), (768, 256))
-FUSED_FROM = 768
+VECTOR_ADDS_FROM = 768
 
 LANDING_BUFS = 10
 PICKED_BUFS = 4
-TOKEN_BANKS = 4
+TURN_BANKS = 4
 
 FLOPS = 2 * SLOTS * (2 * K * H + H * N)
 BYTES = 4 * (K * T + 2 * E * K * H + E * H * N + TOP * T + N * T) + (1 + TOP) * 2 * P * (T // LIST)
@@ -115,7 +115,7 @@ def tile_moe_ecr_glu_sigmoid_kernel(
                     positions.append(load_list((pos1, pos2, pos3, pos4)[e], "positions%d" % e))
             w2_raw = [load_rows(landing, w2[e], "w2_raw", E) for e in range(E)]
             for t0, width in CHUNKS:
-                for r in range(0, TOP, 2):
+                for r in reversed(range(0, TOP, 2)):
                     rows = gate[r : r + 2, 0:P, t0 : t0 + width].rearrange("r p t -> p r t")
                     nc.sync.dma_start(out=gates[t0][:, r : r + 2, :], in_=rows)
 
@@ -217,47 +217,51 @@ def tile_moe_ecr_glu_sigmoid_kernel(
             for odd in range(2):
                 nc.scalar.copy(out=by_expert[1][:, odd, :, :], in_=y_sums[1, odd][:])
 
-        with tc.tile_pool(name="combine", bufs=4) as work, tc.psum_pool(name="turns", bufs=2) as psum:
+        with tc.tile_pool(name="combine", bufs=4) as work, tc.psum_pool(name="turns", bufs=TURN_BANKS) as psum:
             steps = []
             for t0, width in CHUNKS:
-                order = [(r, nb) for r in range(TOP) for nb in range(ROW_BLOCKS)]
                 if t0 == 0:
-                    order = [(r, nb) for nb in range(ROW_BLOCKS) for r in range(TOP)]
-                steps.extend((t0, width, r, nb) for r, nb in order)
-            by_token, by_row, fourth = {}, {}, {}
+                    steps.extend((t0, width, term, nb) for nb in range(ROW_BLOCKS) for term in range(TOP))
+                else:
+                    steps.extend((t0, width, term, nb) for term in range(TOP) for nb in range(ROW_BLOCKS))
+            by_token, by_row, last_products = {}, {}, {}
 
-            for t0, width, r, nb in steps:
+            def store(result, nb, t0, width):
+                nc.sync.dma_start(out=out[nb * P : (nb + 1) * P, t0 : t0 + width], in_=result[:])
+
+            for t0, width, term, nb in steps:
+                r = TOP - 1 - term
                 blocks = [slice(b, b + P) for b in range(0, width, P)]
-                turned_lists = TOP - 1 if t0 >= FUSED_FROM else TOP
+                turned_terms = TOP - 1 if t0 >= VECTOR_ADDS_FROM else TOP
                 entries = positions[r][:, t0 // LIST : (t0 + width) // LIST]
                 picked = work.tile([P, width], F32, name="picked", bufs=PICKED_BUFS)
                 nc.vector.tensor_tensor(picked[:], y[nb][:].indirect(entries), gates[t0][:, r, :], MULT)
-                if r == 0:
-                    by_token[nb] = psum.tile([P, width], F32, name="by_token", bufs=TOKEN_BANKS)
-                if r < turned_lists:
+                if term == 0:
+                    by_token[nb] = psum.tile([P, width], F32, name="by_token")
+                if term < turned_terms:
                     for block in blocks:
                         nc.tensor.matmul(
                             by_token[nb][:, block],
                             picked[:, block],
                             identity[:],
-                            start=(r == 0 and block == blocks[0]),
-                            stop=(r == turned_lists - 1 and block == blocks[-1]),
+                            start=(term == 0 and block == blocks[0]),
+                            stop=(term == turned_terms - 1 and block == blocks[-1]),
                             is_transpose=True,
                         )
-                if r == turned_lists - 1:
+                else:
+                    last_products[nb] = picked
+                if term == turned_terms - 1:
                     summed = work.tile([P, width], F32, name="summed")
                     nc.scalar.copy(out=summed[:], in_=by_token[nb][:])
-                    by_row[nb] = psum.tile([P, width], F32, name="by_row", bufs=4)
+                    by_row[nb] = psum.tile([P, width], F32, name="by_row")
                     for block in blocks:
                         nc.tensor.transpose(by_row[nb][:, block], summed[:, block], identity[:])
-                if r == TOP - 1 and r < turned_lists:
+                if term == TOP - 1 and turned_terms == TOP:
                     result = work.tile([P, width], F32, name="result")
                     nc.scalar.copy(out=result[:], in_=by_row[nb][:])
-                    nc.sync.dma_start(out=out[nb * P : (nb + 1) * P, t0 : t0 + width], in_=result[:])
-                if r == turned_lists:
-                    fourth[nb] = picked
-                if r == turned_lists and nb == ROW_BLOCKS - 1:
-                    for rb in range(ROW_BLOCKS):
+                    store(result, nb, t0, width)
+                if term == turned_terms and nb == ROW_BLOCKS - 1:
+                    for done in range(ROW_BLOCKS):
                         result = work.tile([P, width], F32, name="result")
-                        nc.vector.tensor_tensor(result[:], by_row[rb][:], fourth[rb][:], ADD)
-                        nc.sync.dma_start(out=out[rb * P : (rb + 1) * P, t0 : t0 + width], in_=result[:])
+                        nc.vector.tensor_tensor(result[:], by_row[done][:], last_products[done][:], ADD)
+                        store(result, done, t0, width)

from contextlib import ExitStack

import concourse.mybir as mybir
from concourse.masks import make_identity

K, T, E, C, H, N = 512, 1024, 8, 128, 512, 256
TOP = 4
PAD = 64
SLOTS = E * C

F32 = mybir.dt.float32
BF16 = mybir.dt.bfloat16
U32 = mybir.dt.uint32
U16 = mybir.dt.uint16
U8 = mybir.dt.uint8
FP8X4 = mybir.dt.float8_e4m3fn_x4
SIGMOID = mybir.ActivationFunctionType.Sigmoid
MULT = mybir.AluOpType.mult
ADD = mybir.AluOpType.add

P = 128
PACK = 4
LIST = 16
ROW_BLOCKS = N // P
PAIRS = E // 2

X_PIECE = 512
GATHER = 256
X_ON_SCALAR = 192
W2_ON_SCALAR = 160
LAST_W2_ON_SCALAR = 96
LAST_H_HOST = 2
CHUNKS = ((0, 512), (512, 256), (768, 256))
VECTOR_ADDS_FROM = 768

LANDING_BUFS = 10
PICKED_BUFS = 4
TURN_BANKS = 4

FLOPS = 2 * SLOTS * (2 * K * H + H * N)
BYTES = 4 * (K * T + 2 * E * K * H + E * H * N + TOP * T + N * T) + (1 + TOP) * 2 * P * (T // LIST)


def tile_moe_ecr_glu_sigmoid_kernel(
    tc, xT, w1, w3, w2, gate, offs, pos1, pos2, pos3, pos4, out
):
    nc = tc.nc

    def interleave(grouped, raw, on_scalar):
        shares = ((nc.scalar.copy, 0, on_scalar), (nc.vector.tensor_copy, on_scalar, raw.shape[2]))
        for copy, lo, hi in shares:
            if hi > lo:
                copy(
                    out=grouped[:, lo:hi, :].rearrange("p (c i) j -> p c j i", i=4),
                    in_=raw[:, :, lo:hi].rearrange("p j (c i) -> p c j i", i=4),
                )

    def quantize(grouped, words, scales):
        nc.vector.quantize_mx(
            out=words.bitcast(FP8X4), scales=scales, in_=grouped.rearrange("p w j -> p (w j)")
        )

    def product(sums, stationary, moving):
        nc.tensor.matmul_mx(
            out=sums,
            lhsT=stationary[0].bitcast(FP8X4),
            lhsT_scale=stationary[1],
            rhs=moving[0].bitcast(FP8X4),
            rhs_scale=moving[1],
            start=True,
            stop=True,
        )

    def columns(operand, first, count):
        return tuple(part[:, first : first + count] for part in operand)

    with ExitStack() as ctx:
        keep = ctx.enter_context(tc.tile_pool(name="keep", bufs=1))
        landing = ctx.enter_context(tc.tile_pool(name="landing", bufs=1))

        identity = keep.tile([P, P], F32)
        make_identity(nc, identity[:])
        token_words = keep.tile([P, T], U32, align_bytes=64)
        token_scales = keep.tile([P, T], U8, align_bytes=64)
        nc.gpsimd.memset(token_scales[:], 0)
        y = [keep.tile([P, SLOTS + PAD], F32, name="y%d" % nb) for nb in range(ROW_BLOCKS)]
        for rows in y:
            nc.gpsimd.memset(rows[:, SLOTS:], 0.0)
        gates = {t0: keep.tile([P, TOP, width], F32, name="gate%d" % t0) for t0, width in CHUNKS}

        def load_list(source, name):
            tile = keep.tile([P, T // LIST], U16, name=name)
            nc.sync.dma_start(tile[:], source)
            return tile

        def load_rows(pool, rows, tag, bufs):
            raw = pool.tile([P, PACK, rows.shape[1]], F32, name=tag, bufs=bufs, align_bytes=64)
            nc.sync.dma_start(out=raw[:], in_=rows.rearrange("(p j) w -> p j w", j=PACK))
            return raw

        with tc.tile_pool(name="layers", bufs=3) as work, tc.psum_pool(name="sums", bufs=2) as psum:

            def new_operand(pool, width, tag, bufs):
                words = pool.tile([P, width], U32, name=tag + "_words", bufs=bufs, align_bytes=64)
                scales = pool.tile([P, width], U8, name=tag + "_scales", bufs=bufs, align_bytes=64)
                return words[:], scales[:]

            x_raw = load_rows(work, xT, "x_raw", 1)
            offsets = load_list(offs, "offsets")
            w1_raw, w3_raw, positions = [], [], []
            for e in range(E):
                w1_raw.append(load_rows(landing, w1[e], "w13_raw", LANDING_BUFS))
                w3_raw.append(load_rows(landing, w3[e], "w13_raw", LANDING_BUFS))
                if e < TOP:
                    positions.append(load_list((pos1, pos2, pos3, pos4)[e], "positions%d" % e))
            w2_raw = [load_rows(landing, w2[e], "w2_raw", E) for e in range(E)]
            for t0, width in CHUNKS:
                for r in reversed(range(0, TOP, 2)):
                    rows = gate[r : r + 2, 0:P, t0 : t0 + width].rearrange("r p t -> p r t")
                    nc.sync.dma_start(out=gates[t0][:, r : r + 2, :], in_=rows)

            pieces = [slice(t0, t0 + X_PIECE) for t0 in range(0, T, X_PIECE)]
            x_grouped = [work.tile([P, X_PIECE, PACK], BF16, name="grouped", align_bytes=64) for piece in pieces]
            for piece, grouped in zip(pieces, x_grouped):
                interleave(grouped, x_raw[:, :, piece], X_ON_SCALAR)
            for piece, grouped in zip(pieces, x_grouped):
                quantize(grouped[:], token_words[:, piece], token_scales[:, piece])

            slot_operands, first_sums, turned, pair_inputs, pairs, y_sums = [], {}, {}, {}, {}, {}

            def gather_slots(first):
                entries = offsets[:, first // LIST : (first + GATHER) // LIST]
                words, scales = new_operand(keep, GATHER, "slots%d" % first, 1)
                nc.vector.tensor_copy(words, token_words[:].indirect(entries))
                nc.vector.tensor_copy(scales, token_scales[:].indirect(entries))
                slot_operands.append((words, scales))

            def first_layer(e, grouped):
                weights = new_operand(work, 2 * H, "w13", 3)
                quantize(grouped[:], *weights)
                slots = columns(slot_operands[e * C // GATHER], e * C % GATHER, C)
                first_sums[e] = [psum.tile([C, H], F32, name=tag) for tag in ("a_sum", "b_sum")]
                for i, bank in enumerate(first_sums[e]):
                    product(bank[:], slots, columns(weights, i * H, H))

            def hidden(e):
                if e + 1 < E:
                    sig = w1_raw[e + 1][:, 0, :]
                    h_pairs = w3_raw[e + 1][:, 0, 0 : H // 2]
                else:
                    sig = work.tile([C, H], F32, name="last_sig", bufs=1)[:]
                    h_pairs = w2_raw[LAST_H_HOST][:, 0, :]
                a_sum, b_sum = first_sums[e]
                nc.scalar.activation(sig, a_sum[:], SIGMOID)
                nc.vector.tensor_tensor(h_pairs.bitcast(BF16), b_sum[:], sig, MULT)
                turned[e] = psum.tile([P, 2, C], F32, name="turned")
                for u in range(2):
                    nc.tensor.transpose(turned[e][:, u, :], h_pairs[:, u : H // 2 : 2], identity[:])

            def pair_input(pair):
                if pair not in pair_inputs:
                    if 2 * pair + 3 < E:
                        pair_inputs[pair] = w1_raw[2 * pair + 3][:, 1:3, :].rearrange("p j w -> p (j w)")
                    else:
                        pair_inputs[pair] = work.tile([P, 2 * H], F32, name="last_pair", bufs=1, align_bytes=64)[:]
                return pair_inputs[pair]

            def place_hidden(e):
                first = 2 * (N + e % 2 * C)
                nc.scalar.copy(
                    out=pair_input(e // 2)[:, first : first + 2 * C].rearrange("p (c u) -> p c u", u=2),
                    in_=turned[e][:].rearrange("p u c -> p c u"),
                )

            def second_layer(e):
                on_scalar = W2_ON_SCALAR if e < E - 1 else LAST_W2_ON_SCALAR
                if e % 2 == 0:
                    grouped = pair_input(e // 2).bitcast(BF16).rearrange("p (w j) -> p w j", j=PACK)
                    interleave(grouped[:, 0:N, :], w2_raw[e], on_scalar)
                    weights = pairs[e // 2] = new_operand(work, N + 2 * C, "pair", 2)
                else:
                    grouped = work.tile([P, N, PACK], BF16, name="w2_grouped", align_bytes=64)[:]
                    interleave(grouped, w2_raw[e], on_scalar)
                    weights = new_operand(work, N, "w2", 2)
                quantize(grouped, *weights)
                for nb in range(ROW_BLOCKS):
                    sums = last_sum[:] if (e, nb) == (E - 1, 0) else y_sums[nb, e % 2][:, e // 2, :]
                    product(sums, columns(weights, nb * P, P), columns(pairs[e // 2], N + e % 2 * C, C))

            for e in range(E):
                if e * C % GATHER == 0:
                    gather_slots(e * C)
                grouped = work.tile([P, 2 * H, PACK], BF16, name="grouped", align_bytes=64)
                interleave(grouped[:, 0:H, :], w1_raw[e], H)
                interleave(grouped[:, H : 2 * H, :], w3_raw[e], 0)
                if e >= 1:
                    hidden(e - 1)
                if e >= 3 and e % 2 == 1:
                    place_hidden(e - 3)
                    place_hidden(e - 2)
                first_layer(e, grouped)
            place_hidden(E - 2)

            for odd in range(2):
                y_sums[0, odd] = psum.tile([P, PAIRS - odd, C], F32, name="y_sum%d" % odd, bufs=1)
                y_sums[1, odd] = psum.tile([P, PAIRS, C], F32, name=("a_sum", "b_sum")[odd])
            last_sum = psum.tile([P, C], F32, name="turned")
            for e in range(E):
                second_layer(e)
                if e == LAST_H_HOST:
                    hidden(E - 1)
                    place_hidden(E - 1)
            by_expert = [rows[:, 0:SLOTS].rearrange("p (pair odd c) -> p odd pair c", odd=2, c=C) for rows in y]
            nc.scalar.copy(out=by_expert[0][:, 1, 0 : PAIRS - 1, :], in_=y_sums[0, 1][:])
            nc.scalar.copy(out=by_expert[0][:, 0, :, :], in_=y_sums[0, 0][:])
            nc.vector.tensor_copy(out=y[0][:, SLOTS - C : SLOTS], in_=last_sum[:])
            for odd in range(2):
                nc.scalar.copy(out=by_expert[1][:, odd, :, :], in_=y_sums[1, odd][:])

        with tc.tile_pool(name="combine", bufs=4) as work, tc.psum_pool(name="turns", bufs=TURN_BANKS) as psum:
            steps = []
            for t0, width in CHUNKS:
                if t0 == 0:
                    steps.extend((t0, width, term, nb) for nb in range(ROW_BLOCKS) for term in range(TOP))
                else:
                    steps.extend((t0, width, term, nb) for term in range(TOP) for nb in range(ROW_BLOCKS))
            by_token, by_row, last_products = {}, {}, {}

            def store(result, nb, t0, width):
                nc.sync.dma_start(out=out[nb * P : (nb + 1) * P, t0 : t0 + width], in_=result[:])

            for t0, width, term, nb in steps:
                r = TOP - 1 - term
                blocks = [slice(b, b + P) for b in range(0, width, P)]
                turned_terms = TOP - 1 if t0 >= VECTOR_ADDS_FROM else TOP
                entries = positions[r][:, t0 // LIST : (t0 + width) // LIST]
                picked = work.tile([P, width], F32, name="picked", bufs=PICKED_BUFS)
                nc.vector.tensor_tensor(picked[:], y[nb][:].indirect(entries), gates[t0][:, r, :], MULT)
                if term == 0:
                    by_token[nb] = psum.tile([P, width], F32, name="by_token")
                if term < turned_terms:
                    for block in blocks:
                        nc.tensor.matmul(
                            by_token[nb][:, block],
                            picked[:, block],
                            identity[:],
                            start=(term == 0 and block == blocks[0]),
                            stop=(term == turned_terms - 1 and block == blocks[-1]),
                            is_transpose=True,
                        )
                else:
                    last_products[nb] = picked
                if term == turned_terms - 1:
                    summed = work.tile([P, width], F32, name="summed")
                    nc.scalar.copy(out=summed[:], in_=by_token[nb][:])
                    by_row[nb] = psum.tile([P, width], F32, name="by_row")
                    for block in blocks:
                        nc.tensor.transpose(by_row[nb][:, block], summed[:, block], identity[:])
                if term == TOP - 1 and turned_terms == TOP:
                    result = work.tile([P, width], F32, name="result")
                    nc.scalar.copy(out=result[:], in_=by_row[nb][:])
                    store(result, nb, t0, width)
                if term == turned_terms and nb == ROW_BLOCKS - 1:
                    for done in range(ROW_BLOCKS):
                        result = work.tile([P, width], F32, name="result")
                        nc.vector.tensor_tensor(result[:], by_row[done][:], last_products[done][:], ADD)
                        store(result, done, t0, width)
